import numpy as np, ml_dtypes
CORES = [24,25,26,27,28,29,30,31,224,225,226,227,228,229,230,231]
N = 16
TK, LAY = 128, 4
def setup_inputs(rng):
    return {"x": rng.standard_normal((N, 128, TK), dtype=np.float32).astype(ml_dtypes.bfloat16), "w": (rng.standard_normal((N, 128, LAY * 256), dtype=np.float32) / 16).astype(ml_dtypes.bfloat16)}
def setup_inputs_big(rng):
    d = setup_inputs(rng)
    for k in ("x",): d[k] = (d[k].astype(np.float32) * 1048576.0).astype(d[k].dtype)
    return d
def setup_inputs_small(rng):
    d = setup_inputs(rng)
    for k in ("x",): d[k] = (d[k].astype(np.float32) * (1 / 1048576.0)).astype(d[k].dtype)
    return d
def setup_inputs_apart(rng):
    d = setup_inputs(rng)
    f = (10.0 ** rng.permutation(np.linspace(-1.5, 1.5, N))).astype(np.float32).reshape(N, 1, 1)
    for k in ("x",): d[k] = (d[k].astype(np.float32) * f).astype(d[k].dtype)
    return d
def reference(x, w):
    X, W = x.astype(np.float64), w.astype(np.float64)
    h = list(X)
    for l in range(LAY):
        h = [np.maximum(W[r][:, 256 * l:256 * l + 128].T @ h[r] + W[r][:, 256 * l + 128:256 * l + 256].T @ h[r ^ (1 << l)], 0.0) for r in range(N)]
    return {"y": np.stack(h).astype(ml_dtypes.bfloat16)}

@@ -1,0 +1,184 @@
+from concourse.bass import DstId, RemoteDMATransfer
+from concourse.mybir import AluOpType
+
+D = 128
+
+SCRATCH = {
+    "xs": ("sbuf", [128, 4 * D], "bfloat16"),
+    "wl": ("sbuf", [128, 8 * D], "bfloat16"),
+    "wc": ("sbuf", [128, 6 * D], "bfloat16"),
+    "h1": ("sbuf", [128, 2 * D], "bfloat16"),
+    "h2": ("sbuf", [128, 2 * D], "bfloat16"),
+    "h2p": ("sbuf", [128, 2 * D], "bfloat16"),
+    "h3": ("sbuf", [128, 2 * D], "bfloat16"),
+    "h3o": ("sbuf", [128, D], "bfloat16"),
+    "h3x": ("sbuf", [128, D], "bfloat16"),
+    "yo": ("sbuf", [128, D], "bfloat16"),
+    "zero": ("sbuf", [128, D], "float32"),
+    "p0c": ("psum", [128, 512], "float32"), "p0o": ("psum", [128, 512], "float32"),
+    "p1c": ("psum", [128, 512], "float32"), "p1o": ("psum", [128, 512], "float32"),
+    "p2c": ("psum", [128, 512], "float32"), "p2o": ("psum", [128, 512], "float32"),
+    "p3": ("psum", [128, 512], "float32"),
+}
+SEMAPHORES = ["ldx", "ldw0", "ldw1", "zs", "st", "sent",
+              "xarr", "wa", "wb", "h2a", "h3oa", "h3xa",
+              "t0c", "t0o", "t1c", "t1o", "t2c", "t2o", "t3",
+              "v0c", "v0o", "v1c", "v1o", "v2c", "v2o", "v3"]
+
+
+def _engines(mask):
+    return [b for b in range(mask.bit_length()) if (mask >> b) & 1]
+
+
+def _pack(bits):
+    return sum(1 << b for b in bits)
+
+
+def rank_program(g, core, T, topo):
+    rank = T.rank_of(core)
+    if rank is None:
+        return
+    cores, S = T.cores, T.sem
+    lay = len(cores).bit_length() - 1
+    top = 1 << (lay - 1)
+
+    def carrier(q):
+        return topo.may_write(cores[q], cores[q ^ top])
+
+    fold = [b for b in range(lay - 1) if all(carrier(q) != carrier(q ^ (1 << b)) for q in range(len(cores)))][0]
+    assert lay == 4 and fold == 1
+
+    def slot(q):
+        j = (q & 1) | (((q >> fold) & 1) << 1)
+        return slice(j * D, (j + 1) * D)
+
+    def u(w, l):
+        return w[:, 2 * l * D:(2 * l + 1) * D]
+
+    def v(w, l):
+        return w[:, (2 * l + 1) * D:(2 * l + 2) * D]
+
+    def dst(q):
+        rid, pid = topo.addr(cores[q], core)
+        return DstId(rid=rid, pnc=pid)
+
+    def mask(q):
+        return topo.mask(core, cores[q])
+
+    def n_eng(m):
+        return len(_engines(m))
+
+    C, O = slice(0, D), slice(D, 2 * D)
+    te, ve = g.tensor, g.vector
+    sent = [0]
+
+    def mm(p, lhsT, rhs, start, stop, sem):
+        te.matmul(p[:, 0:D], lhsT, rhs, start, stop).then_inc(sem, 1)
+
+    def relu(out, p, tsem, vsem):
+        ve.wait_ge(tsem, 2)
+        ve.tensor_tensor(out, p[:, 0:D], T.zero[:], AluOpType.max).then_inc(vsem, 1)
+
+    def write(out, in_, q, sem):
+        rid, pid = topo.addr(cores[q], core)
+        g.remote_dma(out, in_, sem, S.sent, pid, rid, mask(q))
+        sent[0] += n_eng(mask(q))
+
+    def deal(q):
+        c = q ^ (1 << fold)
+        off = _engines(topo.mask(cores[q], cores[q ^ top]) & topo.mask(cores[q], cores[c ^ top]))
+        on = [b for b in _engines(topo.mask(cores[q], cores[c])) if b not in off]
+        return off[:len(off) // 2], off[len(off) // 2:], on
+
+    g.sync.dma_start(T.xs[:, slot(rank)], T.x[:]).then_inc(S.ldx, 16)
+    g.scalar.dma_start(T.wl[:, 0:4 * D], T.w[:, 0:4 * D]).then_inc(S.ldw0, 16)
+    g.sync.dma_start(T.wl[:, 4 * D:8 * D], T.w[:, 4 * D:8 * D]).then_inc(S.ldw1, 16)
+    ve.memset(T.zero[:], 0.0).then_inc(S.zs, 1)
+    ve.wait_ge(S.zs, 1)
+
+    if not carrier(rank):
+        r = rank ^ (1 << fold)
+        m = mask(r) & mask(r ^ 1)
+        g.wait_ge(S.ldx, 16)
+        g.remote_dma_fused([RemoteDMATransfer(dst_ids=[dst(r), dst(r ^ 1)], dma_engine_mask=m, remote_sem=S.xarr,
+                                              srcs=[T.xs[:, slot(rank)]],
+                                              dsts=[T.xs[:, slot(rank)], T.xs[:, slot(rank)]])], local_sem=S.sent)
+        sent[0] += n_eng(m)
+        g.wait_ge(S.ldw0, 16)
+        write(T.wc[:, 0:4 * D], T.wl[:, 0:4 * D], r, S.wa)
+        g.wait_ge(S.ldw1, 16)
+        write(T.wc[:, 4 * D:6 * D], T.wl[:, 4 * D:6 * D], r, S.wb)
+
+        te.wait_ge(S.ldw1, 16)
+        te.wait_ge(S.h3oa, len(deal(r)[2]))
+        mm(T.p3, u(T.wl, 3), T.h3o[:], True, False, S.t3)
+        te.wait_ge(S.h3xa, len(deal(r ^ top)[0]))
+        mm(T.p3, v(T.wl, 3), T.h3x[:], False, True, S.t3)
+    else:
+        r, c = rank, rank ^ (1 << fold)
+        g.wait_ge(S.ldx, 16)
+        write(T.xs[:, slot(r)], T.xs[:, slot(r)], r ^ 1, S.xarr)
+
+        n_x = n_eng(topo.mask(cores[r ^ 1], core)) \
+            + n_eng(topo.mask(cores[c], core) & topo.mask(cores[c], cores[r ^ 1])) \
+            + n_eng(topo.mask(cores[c ^ 1], core) & topo.mask(cores[c ^ 1], cores[r ^ 1]))
+        n_w = n_eng(topo.mask(cores[c], core))
+        te.wait_ge(S.ldx, 16)
+        te.wait_ge(S.ldw0, 16)
+        te.wait_ge(S.xarr, n_x)
+        mm(T.p0o, u(T.wl, 0), T.xs[:, slot(r)], True, False, S.t0o)
+        mm(T.p0o, v(T.wl, 0), T.xs[:, slot(r ^ 1)], False, True, S.t0o)
+        te.wait_ge(S.wa, n_w)
+        mm(T.p0c, u(T.wc, 0), T.xs[:, slot(c)], True, False, S.t0c)
+        mm(T.p0c, v(T.wc, 0), T.xs[:, slot(c ^ 1)], False, True, S.t0c)
+        relu(T.h1[:, O], T.p0o, S.t0o, S.v0o)
+        relu(T.h1[:, C], T.p0c, S.t0c, S.v0c)
+
+        te.wait_ge(S.v0o, 1)
+        mm(T.p1o, u(T.wl, 1), T.h1[:, O], True, False, S.t1o)
+        mm(T.p1c, v(T.wc, 1), T.h1[:, O], True, False, S.t1c)
+        te.wait_ge(S.v0c, 1)
+        mm(T.p1c, u(T.wc, 1), T.h1[:, C], False, True, S.t1c)
+        mm(T.p1o, v(T.wl, 1), T.h1[:, C], False, True, S.t1o)
+        relu(T.h2[:, C], T.p1c, S.t1c, S.v1c)
+        relu(T.h2[:, O], T.p1o, S.t1o, S.v1o)
+
+        g.wait_ge(S.v1c, 1)
+        g.wait_ge(S.v1o, 1)
+        write(T.h2p[:], T.h2[:], r ^ 4, S.h2a)
+
+        te.wait_ge(S.ldw1, 16)
+        te.wait_ge(S.wb, n_w)
+        te.wait_ge(S.v1c, 1)
+        mm(T.p2c, u(T.wc, 2), T.h2[:, C], True, False, S.t2c)
+        te.wait_ge(S.v1o, 1)
+        mm(T.p2o, u(T.wl, 2), T.h2[:, O], True, False, S.t2o)
+        te.wait_ge(S.h2a, n_eng(topo.mask(cores[r ^ 4], core)))
+        mm(T.p2c, v(T.wc, 2), T.h2p[:, C], False, True, S.t2c)
+        mm(T.p2o, v(T.wl, 2), T.h2p[:, O], False, True, S.t2o)
+        relu(T.h3[:, C], T.p2c, S.t2c, S.v2c)
+        relu(T.h3[:, O], T.p2o, S.t2o, S.v2o)
+
+        e_c, e_o, e_on = deal(r)
+        g.wait_ge(S.v2c, 1)
+        g.wait_ge(S.v2o, 1)
+        g.remote_dma_fused([
+            RemoteDMATransfer(dst_ids=[dst(c ^ top)], dma_engine_mask=_pack(e_c), remote_sem=S.h3xa,
+                              src=T.h3[:, C], dst=T.h3x[:]),
+            RemoteDMATransfer(dst_ids=[dst(r ^ top)], dma_engine_mask=_pack(e_o), remote_sem=S.h3xa,
+                              src=T.h3[:, O], dst=T.h3x[:]),
+            RemoteDMATransfer(dst_ids=[dst(c)], dma_engine_mask=_pack(e_on), remote_sem=S.h3oa,
+                              src=T.h3[:, C], dst=T.h3o[:]),
+        ], local_sem=S.sent)
+        sent[0] += len(e_c) + len(e_o) + len(e_on)
+
+        te.wait_ge(S.v2o, 1)
+        mm(T.p3, u(T.wl, 3), T.h3[:, O], True, False, S.t3)
+        te.wait_ge(S.h3xa, len(deal(r ^ top)[1]))
+        mm(T.p3, v(T.wl, 3), T.h3x[:], False, True, S.t3)
+
+    relu(T.yo[:], T.p3, S.t3, S.v3)
+    g.sync.wait_ge(S.v3, 1)
+    g.sync.dma_start(T.y[:], T.yo[:]).then_inc(S.st, 16)
+    g.sync.wait_ge(S.st, 16)
+    g.wait_ge(S.sent, sent[0])

@@ -4,12 +4,14 @@ from concourse.mybir import AluOpType
 D = 128
 
 SCRATCH = {
-    "xs": ("sbuf", [128, 4 * D], "bfloat16"),
+    "xs": ("sbuf", [128, 3 * D], "bfloat16"),
+    "cw": ("sbuf", [128, 7 * D], "bfloat16"),
     "wl": ("sbuf", [128, 8 * D], "bfloat16"),
-    "wc": ("sbuf", [128, 6 * D], "bfloat16"),
+    "wf": ("sbuf", [128, 2 * D], "bfloat16"),
     "h1": ("sbuf", [128, 2 * D], "bfloat16"),
     "h2": ("sbuf", [128, 2 * D], "bfloat16"),
     "h2p": ("sbuf", [128, 2 * D], "bfloat16"),
+    "h2f": ("sbuf", [128, 2 * D], "bfloat16"),
     "h3": ("sbuf", [128, 2 * D], "bfloat16"),
     "h3o": ("sbuf", [128, D], "bfloat16"),
     "h3x": ("sbuf", [128, D], "bfloat16"),
@@ -18,12 +20,12 @@ SCRATCH = {
     "p0c": ("psum", [128, 512], "float32"), "p0o": ("psum", [128, 512], "float32"),
     "p1c": ("psum", [128, 512], "float32"), "p1o": ("psum", [128, 512], "float32"),
     "p2c": ("psum", [128, 512], "float32"), "p2o": ("psum", [128, 512], "float32"),
-    "p3": ("psum", [128, 512], "float32"),
+    "p2f": ("psum", [128, 512], "float32"), "p3": ("psum", [128, 512], "float32"),
 }
 SEMAPHORES = ["ldx", "ldw0", "ldw1", "zs", "st", "sent",
-              "xarr", "wa", "wb", "h2a", "h3oa", "h3xa",
-              "t0c", "t0o", "t1c", "t1o", "t2c", "t2o", "t3",
-              "v0c", "v0o", "v1c", "v1o", "v2c", "v2o", "v3"]
+              "xo", "xc", "wa", "wb", "wfa", "h2ca", "h2oa", "hf", "h3oa", "h3xa",
+              "t0c", "t0o", "t1c", "t1o", "t2c", "t2o", "t2f", "t3",
+              "v0c", "v0o", "v1c", "v1o", "v2c", "v2o", "v2f", "v3"]
 
 
 def _engines(mask):
@@ -41,6 +43,7 @@ def rank_program(g, core, T, topo):
     cores, S = T.cores, T.sem
     lay = len(cores).bit_length() - 1
     top = 1 << (lay - 1)
+    sec = top >> 1
 
     def carrier(q):
         return topo.may_write(cores[q], cores[q ^ top])
@@ -48,25 +51,24 @@ def rank_program(g, core, T, topo):
     fold = [b for b in range(lay - 1) if all(carrier(q) != carrier(q ^ (1 << b)) for q in range(len(cores)))][0]
     assert lay == 4 and fold == 1
 
-    def slot(q):
-        j = (q & 1) | (((q >> fold) & 1) << 1)
-        return slice(j * D, (j + 1) * D)
+    def u(l):
+        return T.wl[:, 2 * l * D:(2 * l + 1) * D]
 
-    def u(w, l):
-        return w[:, 2 * l * D:(2 * l + 1) * D]
+    def v(l):
+        return T.wl[:, (2 * l + 1) * D:(2 * l + 2) * D]
 
-    def v(w, l):
-        return w[:, (2 * l + 1) * D:(2 * l + 2) * D]
+    def uc(l):
+        return T.cw[:, (2 * l + 1) * D:(2 * l + 2) * D]
+
+    def vc(l):
+        return T.cw[:, (2 * l + 2) * D:(2 * l + 3) * D]
 
     def dst(q):
         rid, pid = topo.addr(cores[q], core)
         return DstId(rid=rid, pnc=pid)
 
-    def mask(q):
-        return topo.mask(core, cores[q])
-
-    def n_eng(m):
-        return len(_engines(m))
+    def n_eng(a, b):
+        return len(_engines(topo.mask(cores[a], cores[b])))
 
     C, O = slice(0, D), slice(D, 2 * D)
     te, ve = g.tensor, g.vector
@@ -79,103 +81,111 @@ def rank_program(g, core, T, topo):
         ve.wait_ge(tsem, 2)
         ve.tensor_tensor(out, p[:, 0:D], T.zero[:], AluOpType.max).then_inc(vsem, 1)
 
-    def write(out, in_, q, sem):
+    def write(out, in_, q, sem, eng=None):
         rid, pid = topo.addr(cores[q], core)
-        g.remote_dma(out, in_, sem, S.sent, pid, rid, mask(q))
-        sent[0] += n_eng(mask(q))
+        e = _engines(topo.mask(core, cores[q])) if eng is None else eng
+        g.remote_dma(out, in_, sem, S.sent, pid, rid, _pack(e))
+        sent[0] += len(e)
 
     def deal(q):
         c = q ^ (1 << fold)
         off = _engines(topo.mask(cores[q], cores[q ^ top]) & topo.mask(cores[q], cores[c ^ top]))
         on = [b for b in _engines(topo.mask(cores[q], cores[c])) if b not in off]
-        return off[:len(off) // 2], off[len(off) // 2:], on
+        return off, on
 
-    g.sync.dma_start(T.xs[:, slot(rank)], T.x[:]).then_inc(S.ldx, 16)
-    g.scalar.dma_start(T.wl[:, 0:4 * D], T.w[:, 0:4 * D]).then_inc(S.ldw0, 16)
-    g.sync.dma_start(T.wl[:, 4 * D:8 * D], T.w[:, 4 * D:8 * D]).then_inc(S.ldw1, 16)
     ve.memset(T.zero[:], 0.0).then_inc(S.zs, 1)
     ve.wait_ge(S.zs, 1)
 
     if not carrier(rank):
         r = rank ^ (1 << fold)
-        m = mask(r) & mask(r ^ 1)
+        g.sync.dma_start(T.cw[:, 0:D], T.x[:]).then_inc(S.ldx, 16)
+        g.scalar.dma_start(T.cw[:, D:5 * D], T.w[:, 0:4 * D]).then_inc(S.ldw0, 16)
+        g.sync.dma_start(T.wl[:, 4 * D:8 * D], T.w[:, 4 * D:8 * D]).then_inc(S.ldw1, 16)
         g.wait_ge(S.ldx, 16)
-        g.remote_dma_fused([RemoteDMATransfer(dst_ids=[dst(r), dst(r ^ 1)], dma_engine_mask=m, remote_sem=S.xarr,
-                                              srcs=[T.xs[:, slot(rank)]],
-                                              dsts=[T.xs[:, slot(rank)], T.xs[:, slot(rank)]])], local_sem=S.sent)
-        sent[0] += n_eng(m)
+        write(T.xs[:, 2 * D:3 * D], T.cw[:, 0:D], r ^ 1, S.xc)
         g.wait_ge(S.ldw0, 16)
-        write(T.wc[:, 0:4 * D], T.wl[:, 0:4 * D], r, S.wa)
+        write(T.cw[:, 0:5 * D], T.cw[:, 0:5 * D], r, S.wa)
         g.wait_ge(S.ldw1, 16)
-        write(T.wc[:, 4 * D:6 * D], T.wl[:, 4 * D:6 * D], r, S.wb)
+        write(T.cw[:, 5 * D:7 * D], T.wl[:, 4 * D:6 * D], r, S.wb)
 
         te.wait_ge(S.ldw1, 16)
-        te.wait_ge(S.h3oa, len(deal(r)[2]))
-        mm(T.p3, u(T.wl, 3), T.h3o[:], True, False, S.t3)
+        te.wait_ge(S.h3oa, len(deal(r)[1]))
+        mm(T.p3, u(3), T.h3o[:], True, False, S.t3)
         te.wait_ge(S.h3xa, len(deal(r ^ top)[0]))
-        mm(T.p3, v(T.wl, 3), T.h3x[:], False, True, S.t3)
+        mm(T.p3, v(3), T.h3x[:], False, True, S.t3)
     else:
         r, c = rank, rank ^ (1 << fold)
+        off, on = deal(r)
+        g.sync.dma_start(T.xs[:, 0:D], T.x[:]).then_inc(S.ldx, 16)
+        g.scalar.dma_start(T.wl[:, 0:4 * D], T.w[:, 0:4 * D]).then_inc(S.ldw0, 16)
+        g.sync.dma_start(T.wl[:, 4 * D:8 * D], T.w[:, 4 * D:8 * D]).then_inc(S.ldw1, 16)
         g.wait_ge(S.ldx, 16)
-        write(T.xs[:, slot(r)], T.xs[:, slot(r)], r ^ 1, S.xarr)
+        write(T.xs[:, D:2 * D], T.xs[:, 0:D], r ^ 1, S.xo)
+        g.wait_ge(S.ldw1, 16)
+        write(T.wf[:], T.wl[:, 4 * D:6 * D], r ^ top, S.wfa)
 
-        n_x = n_eng(topo.mask(cores[r ^ 1], core)) \
-            + n_eng(topo.mask(cores[c], core) & topo.mask(cores[c], cores[r ^ 1])) \
-            + n_eng(topo.mask(cores[c ^ 1], core) & topo.mask(cores[c ^ 1], cores[r ^ 1]))
-        n_w = n_eng(topo.mask(cores[c], core))
         te.wait_ge(S.ldx, 16)
         te.wait_ge(S.ldw0, 16)
-        te.wait_ge(S.xarr, n_x)
-        mm(T.p0o, u(T.wl, 0), T.xs[:, slot(r)], True, False, S.t0o)
-        mm(T.p0o, v(T.wl, 0), T.xs[:, slot(r ^ 1)], False, True, S.t0o)
-        te.wait_ge(S.wa, n_w)
-        mm(T.p0c, u(T.wc, 0), T.xs[:, slot(c)], True, False, S.t0c)
-        mm(T.p0c, v(T.wc, 0), T.xs[:, slot(c ^ 1)], False, True, S.t0c)
+        mm(T.p0o, u(0), T.xs[:, 0:D], True, False, S.t0o)
+        te.wait_ge(S.xo, n_eng(r ^ 1, r))
+        mm(T.p0o, v(0), T.xs[:, D:2 * D], False, True, S.t0o)
         relu(T.h1[:, O], T.p0o, S.t0o, S.v0o)
+        te.wait_ge(S.wa, n_eng(c, r))
+        mm(T.p0c, uc(0), T.cw[:, 0:D], True, False, S.t0c)
+        te.wait_ge(S.xc, n_eng(c ^ 1, r))
+        mm(T.p0c, vc(0), T.xs[:, 2 * D:3 * D], False, True, S.t0c)
         relu(T.h1[:, C], T.p0c, S.t0c, S.v0c)
-
         te.wait_ge(S.v0o, 1)
-        mm(T.p1o, u(T.wl, 1), T.h1[:, O], True, False, S.t1o)
-        mm(T.p1c, v(T.wc, 1), T.h1[:, O], True, False, S.t1c)
+        mm(T.p1c, vc(1), T.h1[:, O], True, False, S.t1c)
         te.wait_ge(S.v0c, 1)
-        mm(T.p1c, u(T.wc, 1), T.h1[:, C], False, True, S.t1c)
-        mm(T.p1o, v(T.wl, 1), T.h1[:, C], False, True, S.t1o)
+        mm(T.p1c, uc(1), T.h1[:, C], False, True, S.t1c)
+        mm(T.p1o, v(1), T.h1[:, C], True, False, S.t1o)
+        mm(T.p1o, u(1), T.h1[:, O], False, True, S.t1o)
         relu(T.h2[:, C], T.p1c, S.t1c, S.v1c)
         relu(T.h2[:, O], T.p1o, S.t1o, S.v1o)
 
         g.wait_ge(S.v1c, 1)
+        write(T.h2p[:, C], T.h2[:, C], r ^ sec, S.h2ca, on)
         g.wait_ge(S.v1o, 1)
-        write(T.h2p[:], T.h2[:], r ^ 4, S.h2a)
+        g.remote_dma_fused([
+            RemoteDMATransfer(dst_ids=[dst(r ^ sec)], dma_engine_mask=_pack(on), remote_sem=S.h2oa,
+                              src=T.h2[:, O], dst=T.h2p[:, O]),
+            RemoteDMATransfer(dst_ids=[dst(r ^ top), dst(r ^ top ^ sec)], dma_engine_mask=_pack(off), remote_sem=S.hf,
+                              srcs=[T.h2[:, O]], dsts=[T.h2f[:, C], T.h2f[:, O]]),
+        ], local_sem=S.sent)
+        sent[0] += len(on) + len(off)
 
-        te.wait_ge(S.ldw1, 16)
-        te.wait_ge(S.wb, n_w)
+        te.wait_ge(S.wb, n_eng(c, r))
         te.wait_ge(S.v1c, 1)
-        mm(T.p2c, u(T.wc, 2), T.h2[:, C], True, False, S.t2c)
+        mm(T.p2c, uc(2), T.h2[:, C], True, False, S.t2c)
+        te.wait_ge(S.ldw1, 16)
         te.wait_ge(S.v1o, 1)
-        mm(T.p2o, u(T.wl, 2), T.h2[:, O], True, False, S.t2o)
-        te.wait_ge(S.h2a, n_eng(topo.mask(cores[r ^ 4], core)))
-        mm(T.p2c, v(T.wc, 2), T.h2p[:, C], False, True, S.t2c)
-        mm(T.p2o, v(T.wl, 2), T.h2p[:, O], False, True, S.t2o)
+        mm(T.p2o, u(2), T.h2[:, O], True, False, S.t2o)
+        te.wait_ge(S.h2ca, len(deal(r ^ sec)[1]))
+        mm(T.p2c, vc(2), T.h2p[:, C], False, True, S.t2c)
+        te.wait_ge(S.h2oa, len(deal(r ^ sec)[1]))
+        mm(T.p2o, v(2), T.h2p[:, O], False, True, S.t2o)
         relu(T.h3[:, C], T.p2c, S.t2c, S.v2c)
         relu(T.h3[:, O], T.p2o, S.t2o, S.v2o)
 
-        e_c, e_o, e_on = deal(r)
         g.wait_ge(S.v2c, 1)
-        g.wait_ge(S.v2o, 1)
         g.remote_dma_fused([
-            RemoteDMATransfer(dst_ids=[dst(c ^ top)], dma_engine_mask=_pack(e_c), remote_sem=S.h3xa,
+            RemoteDMATransfer(dst_ids=[dst(c ^ top)], dma_engine_mask=_pack(off), remote_sem=S.h3xa,
                               src=T.h3[:, C], dst=T.h3x[:]),
-            RemoteDMATransfer(dst_ids=[dst(r ^ top)], dma_engine_mask=_pack(e_o), remote_sem=S.h3xa,
-                              src=T.h3[:, O], dst=T.h3x[:]),
-            RemoteDMATransfer(dst_ids=[dst(c)], dma_engine_mask=_pack(e_on), remote_sem=S.h3oa,
+            RemoteDMATransfer(dst_ids=[dst(c)], dma_engine_mask=_pack(on), remote_sem=S.h3oa,
                               src=T.h3[:, C], dst=T.h3o[:]),
         ], local_sem=S.sent)
-        sent[0] += len(e_c) + len(e_o) + len(e_on)
+        sent[0] += len(off) + len(on)
 
         te.wait_ge(S.v2o, 1)
-        mm(T.p3, u(T.wl, 3), T.h3[:, O], True, False, S.t3)
-        te.wait_ge(S.h3xa, len(deal(r ^ top)[1]))
-        mm(T.p3, v(T.wl, 3), T.h3x[:], False, True, S.t3)
+        mm(T.p3, u(3), T.h3[:, O], True, False, S.t3)
+        te.wait_ge(S.wfa, n_eng(r ^ top, r))
+        te.wait_ge(S.hf, len(deal(r ^ top)[0]) + len(deal(r ^ top ^ sec)[0]))
+        mm(T.p2f, T.wf[:, C], T.h2f[:, C], True, False, S.t2f)
+        mm(T.p2f, T.wf[:, O], T.h2f[:, O], False, True, S.t2f)
+        relu(T.h3x[:], T.p2f, S.t2f, S.v2f)
+        te.wait_ge(S.v2f, 1)
+        mm(T.p3, v(3), T.h3x[:], False, True, S.t3)
 
     relu(T.yo[:], T.p3, S.t3, S.v3)
     g.sync.wait_ge(S.v3, 1)

from concourse.bass import DstId, RemoteDMATransfer
from concourse.mybir import AluOpType

D = 128

SCRATCH = {
    "xs": ("sbuf", [128, 3 * D], "bfloat16"),
    "cw": ("sbuf", [128, 7 * D], "bfloat16"),
    "wl": ("sbuf", [128, 8 * D], "bfloat16"),
    "wf": ("sbuf", [128, 2 * D], "bfloat16"),
    "h1": ("sbuf", [128, 2 * D], "bfloat16"),
    "h2": ("sbuf", [128, 2 * D], "bfloat16"),
    "h2p": ("sbuf", [128, 2 * D], "bfloat16"),
    "h2f": ("sbuf", [128, 2 * D], "bfloat16"),
    "h3": ("sbuf", [128, 2 * D], "bfloat16"),
    "h3o": ("sbuf", [128, D], "bfloat16"),
    "h3x": ("sbuf", [128, D], "bfloat16"),
    "yo": ("sbuf", [128, D], "bfloat16"),
    "zero": ("sbuf", [128, D], "float32"),
    "p0c": ("psum", [128, 512], "float32"), "p0o": ("psum", [128, 512], "float32"),
    "p1c": ("psum", [128, 512], "float32"), "p1o": ("psum", [128, 512], "float32"),
    "p2c": ("psum", [128, 512], "float32"), "p2o": ("psum", [128, 512], "float32"),
    "p2f": ("psum", [128, 512], "float32"), "p3": ("psum", [128, 512], "float32"),
}
SEMAPHORES = ["ldx", "ldw0", "ldw1", "zs", "st", "sent",
              "xo", "xc", "wa", "wb", "wfa", "h2ca", "h2oa", "hf", "h3oa", "h3xa",
              "t0c", "t0o", "t1c", "t1o", "t2c", "t2o", "t2f", "t3",
              "v0c", "v0o", "v1c", "v1o", "v2c", "v2o", "v2f", "v3"]


def _engines(mask):
    return [b for b in range(mask.bit_length()) if (mask >> b) & 1]


def _pack(bits):
    return sum(1 << b for b in bits)


def rank_program(g, core, T, topo):
    rank = T.rank_of(core)
    if rank is None:
        return
    cores, S = T.cores, T.sem
    lay = len(cores).bit_length() - 1
    top = 1 << (lay - 1)
    sec = top >> 1

    def carrier(q):
        return topo.may_write(cores[q], cores[q ^ top])

    fold = [b for b in range(lay - 1) if all(carrier(q) != carrier(q ^ (1 << b)) for q in range(len(cores)))][0]
    assert lay == 4 and fold == 1

    def u(l):
        return T.wl[:, 2 * l * D:(2 * l + 1) * D]

    def v(l):
        return T.wl[:, (2 * l + 1) * D:(2 * l + 2) * D]

    def uc(l):
        return T.cw[:, (2 * l + 1) * D:(2 * l + 2) * D]

    def vc(l):
        return T.cw[:, (2 * l + 2) * D:(2 * l + 3) * D]

    def dst(q):
        rid, pid = topo.addr(cores[q], core)
        return DstId(rid=rid, pnc=pid)

    def n_eng(a, b):
        return len(_engines(topo.mask(cores[a], cores[b])))

    C, O = slice(0, D), slice(D, 2 * D)
    te, ve = g.tensor, g.vector
    sent = [0]

    def mm(p, lhsT, rhs, start, stop, sem):
        te.matmul(p[:, 0:D], lhsT, rhs, start, stop).then_inc(sem, 1)

    def relu(out, p, tsem, vsem):
        ve.wait_ge(tsem, 2)
        ve.tensor_tensor(out, p[:, 0:D], T.zero[:], AluOpType.max).then_inc(vsem, 1)

    def write(out, in_, q, sem, eng=None):
        rid, pid = topo.addr(cores[q], core)
        e = _engines(topo.mask(core, cores[q])) if eng is None else eng
        g.remote_dma(out, in_, sem, S.sent, pid, rid, _pack(e))
        sent[0] += len(e)

    def deal(q):
        c = q ^ (1 << fold)
        off = _engines(topo.mask(cores[q], cores[q ^ top]) & topo.mask(cores[q], cores[c ^ top]))
        on = [b for b in _engines(topo.mask(cores[q], cores[c])) if b not in off]
        return off, on

    ve.memset(T.zero[:], 0.0).then_inc(S.zs, 1)
    ve.wait_ge(S.zs, 1)

    if not carrier(rank):
        r = rank ^ (1 << fold)
        g.sync.dma_start(T.cw[:, 0:D], T.x[:]).then_inc(S.ldx, 16)
        g.scalar.dma_start(T.cw[:, D:5 * D], T.w[:, 0:4 * D]).then_inc(S.ldw0, 16)
        g.sync.dma_start(T.wl[:, 4 * D:8 * D], T.w[:, 4 * D:8 * D]).then_inc(S.ldw1, 16)
        g.wait_ge(S.ldx, 16)
        write(T.xs[:, 2 * D:3 * D], T.cw[:, 0:D], r ^ 1, S.xc)
        g.wait_ge(S.ldw0, 16)
        write(T.cw[:, 0:5 * D], T.cw[:, 0:5 * D], r, S.wa)
        g.wait_ge(S.ldw1, 16)
        write(T.cw[:, 5 * D:7 * D], T.wl[:, 4 * D:6 * D], r, S.wb)

        te.wait_ge(S.ldw1, 16)
        te.wait_ge(S.h3oa, len(deal(r)[1]))
        mm(T.p3, u(3), T.h3o[:], True, False, S.t3)
        te.wait_ge(S.h3xa, len(deal(r ^ top)[0]))
        mm(T.p3, v(3), T.h3x[:], False, True, S.t3)
    else:
        r, c = rank, rank ^ (1 << fold)
        off, on = deal(r)
        g.sync.dma_start(T.xs[:, 0:D], T.x[:]).then_inc(S.ldx, 16)
        g.scalar.dma_start(T.wl[:, 0:4 * D], T.w[:, 0:4 * D]).then_inc(S.ldw0, 16)
        g.sync.dma_start(T.wl[:, 4 * D:8 * D], T.w[:, 4 * D:8 * D]).then_inc(S.ldw1, 16)
        g.wait_ge(S.ldx, 16)
        write(T.xs[:, D:2 * D], T.xs[:, 0:D], r ^ 1, S.xo)
        g.wait_ge(S.ldw1, 16)
        write(T.wf[:], T.wl[:, 4 * D:6 * D], r ^ top, S.wfa)

        te.wait_ge(S.ldx, 16)
        te.wait_ge(S.ldw0, 16)
        mm(T.p0o, u(0), T.xs[:, 0:D], True, False, S.t0o)
        te.wait_ge(S.xo, n_eng(r ^ 1, r))
        mm(T.p0o, v(0), T.xs[:, D:2 * D], False, True, S.t0o)
        relu(T.h1[:, O], T.p0o, S.t0o, S.v0o)
        te.wait_ge(S.wa, n_eng(c, r))
        mm(T.p0c, uc(0), T.cw[:, 0:D], True, False, S.t0c)
        te.wait_ge(S.xc, n_eng(c ^ 1, r))
        mm(T.p0c, vc(0), T.xs[:, 2 * D:3 * D], False, True, S.t0c)
        relu(T.h1[:, C], T.p0c, S.t0c, S.v0c)
        te.wait_ge(S.v0o, 1)
        mm(T.p1c, vc(1), T.h1[:, O], True, False, S.t1c)
        te.wait_ge(S.v0c, 1)
        mm(T.p1c, uc(1), T.h1[:, C], False, True, S.t1c)
        mm(T.p1o, v(1), T.h1[:, C], True, False, S.t1o)
        mm(T.p1o, u(1), T.h1[:, O], False, True, S.t1o)
        relu(T.h2[:, C], T.p1c, S.t1c, S.v1c)
        relu(T.h2[:, O], T.p1o, S.t1o, S.v1o)

        g.wait_ge(S.v1c, 1)
        write(T.h2p[:, C], T.h2[:, C], r ^ sec, S.h2ca, on)
        g.wait_ge(S.v1o, 1)
        g.remote_dma_fused([
            RemoteDMATransfer(dst_ids=[dst(r ^ sec)], dma_engine_mask=_pack(on), remote_sem=S.h2oa,
                              src=T.h2[:, O], dst=T.h2p[:, O]),
            RemoteDMATransfer(dst_ids=[dst(r ^ top), dst(r ^ top ^ sec)], dma_engine_mask=_pack(off), remote_sem=S.hf,
                              srcs=[T.h2[:, O]], dsts=[T.h2f[:, C], T.h2f[:, O]]),
        ], local_sem=S.sent)
        sent[0] += len(on) + len(off)

        te.wait_ge(S.wb, n_eng(c, r))
        te.wait_ge(S.v1c, 1)
        mm(T.p2c, uc(2), T.h2[:, C], True, False, S.t2c)
        te.wait_ge(S.ldw1, 16)
        te.wait_ge(S.v1o, 1)
        mm(T.p2o, u(2), T.h2[:, O], True, False, S.t2o)
        te.wait_ge(S.h2ca, len(deal(r ^ sec)[1]))
        mm(T.p2c, vc(2), T.h2p[:, C], False, True, S.t2c)
        te.wait_ge(S.h2oa, len(deal(r ^ sec)[1]))
        mm(T.p2o, v(2), T.h2p[:, O], False, True, S.t2o)
        relu(T.h3[:, C], T.p2c, S.t2c, S.v2c)
        relu(T.h3[:, O], T.p2o, S.t2o, S.v2o)

        g.wait_ge(S.v2c, 1)
        g.remote_dma_fused([
            RemoteDMATransfer(dst_ids=[dst(c ^ top)], dma_engine_mask=_pack(off), remote_sem=S.h3xa,
                              src=T.h3[:, C], dst=T.h3x[:]),
            RemoteDMATransfer(dst_ids=[dst(c)], dma_engine_mask=_pack(on), remote_sem=S.h3oa,
                              src=T.h3[:, C], dst=T.h3o[:]),
        ], local_sem=S.sent)
        sent[0] += len(off) + len(on)

        te.wait_ge(S.v2o, 1)
        mm(T.p3, u(3), T.h3[:, O], True, False, S.t3)
        te.wait_ge(S.wfa, n_eng(r ^ top, r))
        te.wait_ge(S.hf, len(deal(r ^ top)[0]) + len(deal(r ^ top ^ sec)[0]))
        mm(T.p2f, T.wf[:, C], T.h2f[:, C], True, False, S.t2f)
        mm(T.p2f, T.wf[:, O], T.h2f[:, O], False, True, S.t2f)
        relu(T.h3x[:], T.p2f, S.t2f, S.v2f)
        te.wait_ge(S.v2f, 1)
        mm(T.p3, v(3), T.h3x[:], False, True, S.t3)

    relu(T.yo[:], T.p3, S.t3, S.v3)
    g.sync.wait_ge(S.v3, 1)
    g.sync.dma_start(T.y[:], T.yo[:]).then_inc(S.st, 16)
    g.sync.wait_ge(S.st, 16)
    g.wait_ge(S.sent, sent[0])
